import numpy as np, ml_dtypes
CORES = [5,29,101,125,133,157,229,253]
N = 8
import mx_ref
BF = ml_dtypes.bfloat16
def decode(q):
    o = []
    for b in range(4):
        e = np.zeros((128, 128, 4), np.float32); e[np.arange(128), np.arange(128), b] = 1
        o.append(mx_ref.matmul(mx_ref.quantize(e.reshape(128, 512).astype(BF)), q))
    return np.stack(o, axis=2).reshape(128, -1)
def cut(t, i, w=512):
    return t[:, w * i:w * i + w]
def f(rng, *shape):
    return mx_ref.flush((rng.standard_normal(shape, dtype=np.float32) * np.exp2(rng.integers(-2, 3, shape[:-1] + (1,)))).astype(BF))
def wide(rng, *shape, cols=0):
    v = rng.standard_normal(shape, dtype=np.float32) * np.exp2(rng.integers(-12, 13, shape)).astype(np.float32)
    if cols: v *= np.repeat(np.exp2(rng.integers(-cols, cols + 1, shape[:-2] + (1, shape[-1] // 4))) * (rng.random(shape[:-2] + (1, shape[-1] // 4)) > 0.0625), 4, axis=-1).astype(np.float32)
    return mx_ref.flush(v.astype(BF))
T, CL, O = 256, 31, 2
def taps(v):
    d = np.zeros((N, 128, 512), BF); d[:, :, :64] = mx_ref.flush(v.astype(np.float32).astype(BF)); return d
def planted(rng, a, *v):
    d = setup_inputs(rng); d["x"] = np.array(d["x"]); t = np.zeros((N, 128, 64))
    for r in range(N):
        rows = rng.permutation(512)[:len(v)]
        for m in range(len(v)):
            p, b = divmod(int(rows[m]), 4)
            d["x"][r, p, b::4] = mx_ref.flush(a[r].astype(BF)); t[r, p, b::4] = v[m][r]
    d["u"] = taps(t); return d
def setup_inputs(rng):
    return {"x": f(rng, N, 128, 4 * T), "u": taps(f(rng, N, 128, 64).astype(np.float32) * np.float32(CL * 0.005)), "w": f(rng, N, 128, 2 * O * 512)}
def setup_inputs_edge(rng):
    a = rng.uniform(-0.25, 0.25, (N, T)); a[:, :CL] = -rng.uniform(0.75, 1.25, (N, CL)); a[:, T - CL:] = rng.uniform(0.75, 1.25, (N, CL))
    return planted(rng, a, rng.uniform(0.5, 1.0, (N, 16)) * CL)
def setup_inputs_halves(rng):
    return planted(rng, rng.choice([-3.0, -1.0, 1.0, 3.0], (N, T)), rng.choice([-2.5, -1.5, -0.5, 0.5, 1.5, 2.5], (N, 16)))
def setup_inputs_last(rng):
    a = rng.choice([-1.0, 1.0], (N, T)); a[:, 0] = -1.0; a[:, T - 1] = 1.0
    return planted(rng, a, np.full((N, 16), CL + 1.0), np.full((N, 16), -1.25))
def setup_inputs_out(rng):
    return planted(rng, np.ones((N, T)), np.tile(np.repeat([-256.0, 256.0], 8), (N, 1)))
def setup_inputs_spread(rng):
    d = setup_inputs(rng); d["x"] = wide(rng, N, 128, 4 * T, cols=8)
    d["u"] = taps(f(rng, N, 128, 64).astype(np.float32) * np.float32(CL * 0.005 * 2.0 ** -10)); return d
def check_inputs(d):
    return ["u"] if (np.asarray(d["u"])[:, :, 64:].astype(np.float32) != 0).any() else []
def reference(x, u, w):
    V = np.concatenate([decode(mx_ref.quantize(x[r])) for r in range(N)], axis=1).reshape(8, 16, N * T, 4)
    y = np.zeros((N, 128, O * T), np.float32)
    for r in range(N):
        o = mx_ref.matmul(mx_ref.quantize(u[r]), mx_ref.quantize(x[r]))[:16]
        o = np.minimum(np.maximum(o, np.float32(-CL)), np.float32(CL))
        n = np.rint(o); fr = o - n
        i = np.clip(r * T + np.arange(T) + n.astype(np.int64), 0, N * T - 1); i1 = np.minimum(i + 1, N * T - 1)
        M = []
        for k in range(2):
            t = np.zeros((8, 16, T, 4), np.float32)
            for g in range(8):
                a, b = V[g][:, i[8 * k + g]], V[g][:, i1[8 * k + g]]
                t[g] = a + fr[8 * k + g][None, :, None] * (b - a)
            M.append(mx_ref.quantize(t.reshape(128, 4 * T).astype(BF)))
        for c in range(O):
            y[r][:, T * c:T * c + T] = mx_ref.matmul(mx_ref.quantize(np.ascontiguousarray(cut(w[r], c))), M[0]) + mx_ref.matmul(mx_ref.quantize(np.ascontiguousarray(cut(w[r], O + c))), M[1])
    return {"y": y}

@@ -1,0 +1,336 @@
+from concourse.bass import DstId, RemoteDMATransfer
+from concourse.mybir import dt, AluOpType, ActivationFunctionType
+
+H = 32
+TC = 256
+CL = 31
+SCRATCH = {
+    "xe": ("sbuf", [128, 512], "bfloat16"),
+    "qe": ("sbuf", [128, 128], "float8_e4m3fn_x4"),
+    "se": ("sbuf", [128, 128], "uint8"),
+    "rq": ("sbuf", [128, H], "float8_e4m3fn_x4"),
+    "rs": ("sbuf", [128, H], "uint8"),
+    "xt": ("sbuf", [128, 1408], "bfloat16"),
+    "qx": ("sbuf", [128, 416], "float8_e4m3fn_x4"),
+    "sx": ("sbuf", [128, 416], "uint8"),
+    "ub": ("sbuf", [128, 2, 8, 4], "bfloat16"),
+    "us": ("sbuf", [128, 2, 8, 16, 4], "bfloat16"),
+    "ss": ("sbuf", [128, 2, 8, 16, 4], "bfloat16"),
+    "qu": ("sbuf", [128, 512], "float8_e4m3fn_x4"),
+    "su": ("sbuf", [128, 512], "uint8"),
+    "one": ("sbuf", [128, 516], "bfloat16"),
+    "eye": ("sbuf", [128, 516], "bfloat16"),
+    "qi": ("sbuf", [128, 512], "float8_e4m3fn_x4"),
+    "si": ("sbuf", [128, 512], "uint8"),
+    "wb": ("sbuf", [128, 2048], "bfloat16"),
+    "qw": ("sbuf", [128, 512], "float8_e4m3fn_x4"),
+    "sw": ("sbuf", [128, 512], "uint8"),
+    "pi": ("sbuf", [128, 1], "int32"),
+    "ti": ("sbuf", [128, 1], "int32"),
+    "h4": ("sbuf", [128, 1], "int32"),
+    "tq": ("sbuf", [128, 1], "float32"),
+    "te": ("sbuf", [128, 1], "float32"),
+    "tl": ("sbuf", [128, 1], "float32"),
+    "hi": ("sbuf", [128, 1], "float32"),
+    "he": ("sbuf", [128, 1], "float32"),
+    "lim": ("sbuf", [128, 1], "float32"),
+    "ic": ("sbuf", [128, 128], "float32"),
+    "tab": ("sbuf", [128, 128], "float32"),
+    "nl": ("sbuf", [128, 128], "int32"),
+    "wl": ("sbuf", [128, 128], "float32"),
+    "lst": ("sbuf", [128, 128], "uint16"),
+    "fa": ("sbuf", [128, 512], "float32"),
+    "fn": ("sbuf", [128, 512], "int32"),
+    "fc": ("sbuf", [128, 512], "float32"),
+    "fx": ("sbuf", [128, 2048], "float32"),
+    "vw": ("sbuf", [128, 1536], "float32"),
+    "dw": ("sbuf", [128, 1536], "float32"),
+    "pr": ("sbuf", [128, 2048], "float32"),
+    "mt": ("sbuf", [128, 2048], "bfloat16"),
+    "qm": ("sbuf", [128, 512], "float8_e4m3fn_x4"),
+    "sm": ("sbuf", [128, 512], "uint8"),
+    "ys": ("sbuf", [128, 512], "float32"),
+    "pf0": ("psum", [128, 512], "float32"),
+    "pf1": ("psum", [128, 512], "float32"),
+    "pl": ("psum", [128, 512], "float32"),
+    "pv0": ("psum", [128, 512], "float32"),
+    "pv1": ("psum", [128, 512], "float32"),
+    "pv2": ("psum", [128, 512], "float32"),
+    "pv3": ("psum", [128, 512], "float32"),
+    "px": ("psum", [128, 512], "float32"),
+}
+SEMAPHORES = (["d_xe", "d_u", "d_x", "d_w", "st1", "st2", "ra", "rb", "arr", "loc", "g_p", "g_e", "g_c"]
+              + ["v_ones", "v_xp", "v_ss", "v_hz", "v_c1", "v_c2", "v_c3", "v_tab", "v_e", "v_qe", "v_u1", "v_u2", "v_u3",
+                 "v_qu", "v_qx", "v_qs", "v_a", "v_n", "v_l1", "v_l2", "v_l3", "v_f", "v_fe", "v_d", "v_qw", "v_p", "v_m",
+                 "v_qm", "v_dl", "v_pe", "v_me", "v_qme", "v_y"]
+              + ["s_ss", "s_vc", "s_x", "s_dc", "s_xe", "s_y", "s_ye"]
+              + ["s_v%d" % b for b in range(4)] + ["s_lv%d" % b for b in range(4)]
+              + ["t_f0", "t_f1", "t_l", "t_oi0", "t_oi1", "t_oe0", "t_oe1"]
+              + ["t_v%d" % b for b in range(4)] + ["t_lv%d" % b for b in range(4)])
+
+
+def mask_of(engines):
+    return sum(1 << e for e in engines)
+
+
+def routes(T, topo, core):
+    r, n = T.rank_of(core), len(T.cores)
+    out = []
+    for side, nb in ((0, r - 1), (1, r + 1)):
+        if not 0 <= nb < n:
+            continue
+        dst = T.cores[nb]
+        cand = [c for c in topo.cores_of(core) if c != core and topo.may_write(c, dst)]
+        cand.sort(key=lambda c: (topo.die(c) != topo.die(core), c))
+        relay = cand[side]
+        near = topo.engines(core, relay)[4 * side:4 * side + 4]
+        far = topo.engines(relay, dst)[::2]
+        land = H if side == 1 or nb == 0 else 0
+        out.append((side, relay, dst, near, far, H * side, land))
+    return out
+
+
+def relay_program(g, core, T, topo):
+    for rc in topo.cores_of(core):
+        if T.rank_of(rc) is None:
+            continue
+        for side, relay, dst, near, far, col, land in routes(T, topo, rc):
+            if relay != core:
+                continue
+            rid, pid = topo.addr(dst, core)
+            m = mask_of(far)
+            g.wait_ge(T.sem.ra, len(near))
+            g.remote_dma(T.qx[:, land:land + H].bitcast(dt.uint8), T.rq[:, 0:H].bitcast(dt.uint8), T.sem.arr, T.sem.loc,
+                         pid, rid, m)
+            g.wait_ge(T.sem.rb, len(near))
+            g.remote_dma(T.sx[:, land:land + H], T.rs[:, 0:H], T.sem.arr, T.sem.loc, pid, rid, m)
+            g.wait_ge(T.sem.loc, 2 * len(far))
+
+
+def rank_program(g, core, T, topo):
+    rank = T.rank_of(core)
+    if rank is None:
+        relay_program(g, core, T, topo)
+        return
+    n = len(T.cores)
+    first, last = rank == 0, rank == n - 1
+    S = T.sem
+    A = AluOpType
+    CP = ActivationFunctionType.Copy
+    V, C, P, Y = g.vector, g.scalar, g.tensor, g.sync
+    pv = [T["pv%d" % b] for b in range(4)]
+    pf = [T.pf0, T.pf1]
+    out = routes(T, topo, core)
+    arrivals = 0
+    for nb in (rank - 1, rank + 1):
+        if 0 <= nb < n:
+            arrivals += sum(2 * len(q[4]) for q in routes(T, topo, T.cores[nb]) if q[2] == core)
+
+    Y.dma_start(T.xe[:, 0:4 * H], T.x[:, 0:4 * H]).then_inc(S.d_xe, 16)
+    C.dma_start(T.xe[:, 4 * H:8 * H], T.x[:, 4 * (TC - H):4 * TC]).then_inc(S.d_xe, 16)
+    Y.dma_start(T.ub[:], T.u[:, 0:64]).then_inc(S.d_u, 16)
+    C.dma_start(T.xt[:, 0:1024], T.x[:]).then_inc(S.d_x, 16)
+    C.dma_start(T.xt[:, 1024:1408], T.x[:, 512:896]).then_inc(S.d_x, 16)
+    Y.wait_ge(S.d_x, 32)
+    Y.dma_start(T.wb[:], T.w[:]).then_inc(S.d_w, 16)
+
+    g.iota(T.pi[:], [[0, 1]], 0, 1).then_inc(S.g_p, 1)
+    g.wait_ge(S.v_ones, 1)
+    g.affine_select(T.eye[:], T.one[:], [[-1, 516]], A.is_equal, 0.0, 4, 4).then_inc(S.g_e, 1)
+    g.iota(T.ic[:], [[1, 128]], 0, 0, allow_small_or_imprecise_dtypes=True).then_inc(S.g_c, 1)
+    g.wait_ge(S.v_qe, 1)
+    codes, planes = [], []
+    for side, relay, dst, near, far, col, land in out:
+        rid, pid = topo.addr(relay, core)
+        to = [DstId(rid=rid, pnc=pid)]
+        codes.append(RemoteDMATransfer(dst_ids=to, dma_engine_mask=mask_of(near), remote_sem=S.ra,
+                                       src=T.qe[:, col:col + H].bitcast(dt.uint8), dst=T.rq[:, 0:H].bitcast(dt.uint8)))
+        planes.append(RemoteDMATransfer(dst_ids=to, dma_engine_mask=mask_of(near), remote_sem=S.rb,
+                                        src=T.se[:, col:col + H], dst=T.rs[:, 0:H]))
+    g.remote_dma_fused(codes, local_sem=S.loc)
+    g.remote_dma_fused(planes, local_sem=S.loc)
+    g.wait_ge(S.loc, sum(2 * len(q[3]) for q in out))
+
+    V.memset(T.one[:], 1.0).then_inc(S.v_ones, 1)
+    V.memset(T.xe[:, 8 * H:512], 0.0).then_inc(S.v_xp, 1)
+    V.memset(T.ss[:], 0.0).then_inc(S.v_ss, 1)
+    gap = (4 * (TC + H - 1), 4 * (TC + 2 * H)) if first else (4 * (TC - 1), 4 * (TC + H))
+    if first or last:
+        V.memset(T.vw[:, gap[0] + 4:gap[1]], 0.0).then_inc(S.v_hz, 1)
+        V.memset(T.dw[:, gap[0]:gap[1]], 0.0).then_inc(S.v_hz, 1)
+    V.wait_ge(S.g_p, 1)
+    V.tensor_scalar(T.ti[:], T.pi[:], 3, None, A.bitwise_and).then_inc(S.v_c1, 1)
+    V.tensor_scalar(T.h4[:], T.pi[:], 4, None, A.bitwise_and).then_inc(S.v_c1, 1)
+    V.wait_ge(S.v_c1, 2)
+    V.tensor_scalar(T.tq[:], T.ti[:], 0.25, None, A.mult).then_inc(S.v_c2, 1)
+    V.tensor_scalar(T.te[:], T.ti[:], 0.25, float(TC + 2 * H), A.mult, A.add).then_inc(S.v_c2, 1)
+    if first or last:
+        V.tensor_scalar(T.tl[:], T.ti[:], 1.0, 4.0 * (TC + 2 * H) if first else 4.0 * (TC - 1) + 4000.0, A.mult,
+                        A.add).then_inc(S.v_c2, 1)
+    V.wait_ge(S.v_c2, 3 if first or last else 2)
+    V.tensor_scalar(T.hi[:], T.h4[:], 24.0, T.tq[:], A.mult, A.add).then_inc(S.v_c3, 1)
+    V.tensor_scalar(T.he[:], T.h4[:], -24.0, T.te[:], A.mult, A.add).then_inc(S.v_c3, 1)
+    if first or last:
+        V.tensor_scalar(T.lim[:], T.h4[:], -1.0 * (TC + 2 * H) if first else -1000.0, T.tl[:], A.mult,
+                        A.add).then_inc(S.v_c3, 1)
+    V.wait_ge(S.g_e, 1)
+    for b in range(4):
+        V.quantize_mx(T.qi[:, 128 * b:128 * b + 128], T.si[:, 128 * b:128 * b + 128],
+                      T.eye[:, 4 - b:516 - b]).then_inc(S.v_e, 1)
+    V.wait_ge(S.v_xp, 1)
+    V.wait_ge(S.d_xe, 32)
+    V.quantize_mx(T.qe[:], T.se[:], T.xe[:]).then_inc(S.v_qe, 1)
+    V.wait_ge(S.d_u, 16)
+    for q in range(4):
+        V.tensor_copy(T.us[:, :, :, q, :], T.ub[:]).then_inc(S.v_u1, 1)
+    V.wait_ge(S.v_u1, 4)
+    V.tensor_copy(T.us[:, :, :, 4:8, :], T.us[:, :, :, 0:4, :]).then_inc(S.v_u2, 1)
+    V.wait_ge(S.v_u2, 1)
+    V.tensor_copy(T.us[:, :, :, 8:16, :], T.us[:, :, :, 0:8, :]).then_inc(S.v_u3, 1)
+    V.wait_ge(S.v_c3, 3 if first or last else 2)
+    V.wait_ge(S.g_c, 1)
+    V.tensor_scalar(T.tab[:, 0:32], T.ic[:, 0:32], T.he[:], None, A.add).then_inc(S.v_tab, 1)
+    V.tensor_scalar(T.tab[:, 32:128], T.ic[:, 32:128], T.hi[:], None, A.add).then_inc(S.v_tab, 1)
+    V.wait_ge(S.v_u3, 1)
+    V.quantize_mx(T.qu[:, 0:256], T.su[:, 0:256], T.us[:]).then_inc(S.v_qu, 1)
+    V.wait_ge(S.d_x, 32)
+    V.quantize_mx(T.qx[:, 64:416], T.sx[:, 64:416], T.xt[:]).then_inc(S.v_qx, 1)
+    V.wait_ge(S.s_ss, 4)
+    V.quantize_mx(T.qu[:, 256:512], T.su[:, 256:512], T.ss[:]).then_inc(S.v_qs, 1)
+    for k in range(2):
+        V.wait_ge(S["t_f%d" % k], 1)
+        V.tensor_scalar(T.fa[:, 256 * k:256 * k + 256], pf[k][:, 0:256], -float(CL), float(CL), A.max,
+                        A.min).then_inc(S.v_a, 1)
+        V.tensor_scalar(T.fn[:, 256 * k:256 * k + 256], pf[k][:, 0:256], -float(CL), float(CL), A.max,
+                        A.min).then_inc(S.v_n, 1)
+    V.wait_ge(S.v_a, 2)
+    V.wait_ge(S.v_n, 2)
+    for sem, c0, c1 in ((S.v_f, 32, 128), (S.v_fe, 0, 32)):
+        for k in range(2):
+            for h in range(2):
+                a = 256 * k + (c0 if h == 0 else (TC - H if c0 == 0 else 128))
+                e = a + c1 - c0
+                V.tensor_tensor(T.fc[:, 4 * c0 + 2 * k + h:4 * c1:4], T.fa[:, a:e], T.fn[:, a:e], A.subtract).then_inc(sem, 1)
+    V.wait_ge(S.t_l, 1)
+    V.tensor_scalar(T.nl[:], T.pl[:, 0:128], -float(CL), float(CL), A.max, A.min).then_inc(S.v_l1, 1)
+    V.wait_ge(S.v_tab, 2)
+    V.wait_ge(S.v_l1, 1)
+    V.tensor_tensor(T.wl[:], T.nl[:], T.tab[:], A.add).then_inc(S.v_l2, 1)
+    for b in range(4):
+        V.wait_ge(S["s_v%d" % b], 1)
+        V.tensor_tensor(T.dw[:, b:1020:4], pv[b][:, 1:256], T.vw[:, b:1020:4], A.subtract).then_inc(S.v_d, 1)
+    V.wait_ge(S.v_l2, 1)
+    if first or last:
+        V.tensor_scalar(T.lst[:, 0:32], T.wl[:, 0:32], 4.0, T.lim[:], A.mult, A.max if first else A.min).then_inc(S.v_l3, 1)
+    else:
+        V.tensor_scalar(T.lst[:, 0:32], T.wl[:, 0:32], 4.0, None, A.mult).then_inc(S.v_l3, 1)
+    V.tensor_scalar(T.lst[:, 32:128], T.wl[:, 32:128], 4.0, None, A.mult).then_inc(S.v_l3, 1)
+    V.wait_ge(S.d_w, 16)
+    V.quantize_mx(T.qw[:], T.sw[:], T.wb[:]).then_inc(S.v_qw, 1)
+    V.wait_ge(S.v_l3, 2)
+    V.wait_ge(S.v_d, 4)
+    V.wait_ge(S.s_x, 4)
+    V.tensor_tensor(T.pr[:, 512:2048], T.dw[:, 0:1020].indirect(T.lst[:, 32:128]), T.fx[:, 512:2048], A.mult).then_inc(S.v_p, 1)
+    V.wait_ge(S.v_p, 1)
+    V.tensor_tensor(T.mt[:, 512:2048], T.vw[:, 0:1020].indirect(T.lst[:, 32:128]), T.pr[:, 512:2048], A.add).then_inc(S.v_m, 1)
+    V.wait_ge(S.v_m, 1)
+    V.quantize_mx(T.qm[:, 128:512], T.sm[:, 128:512], T.mt[:, 512:2048]).then_inc(S.v_qm, 1)
+    if first or last:
+        V.wait_ge(S.v_hz, 2)
+    for b in range(4):
+        V.wait_ge(S["s_lv%d" % b], 1)
+        if last:
+            V.tensor_tensor(T.dw[:, 1152 + b:1280:4], pv[b][:, 1:33], T.vw[:, 1152 + b:1280:4], A.subtract).then_inc(S.v_dl, 1)
+        elif first:
+            V.tensor_tensor(T.dw[:, 1020 + b:1148:4], pv[b][:, 0:32], T.vw[:, 1020 + b:1148:4], A.subtract).then_inc(S.v_dl, 1)
+        else:
+            V.tensor_tensor(T.dw[:, 1020 + b:1280:4], pv[b][:, 0:65], T.vw[:, 1020 + b:1280:4], A.subtract).then_inc(S.v_dl, 1)
+    V.wait_ge(S.s_vc, 1)
+    V.wait_ge(S.s_dc, 1)
+    V.wait_ge(S.s_xe, 4)
+    V.wait_ge(S.v_dl, 4)
+    V.tensor_tensor(T.pr[:, 0:512], T.dw[:].indirect(T.lst[:, 0:32]), T.fx[:, 0:512], A.mult).then_inc(S.v_pe, 1)
+    V.wait_ge(S.v_pe, 1)
+    V.tensor_tensor(T.mt[:, 0:512], T.vw[:].indirect(T.lst[:, 0:32]), T.pr[:, 0:512], A.add).then_inc(S.v_me, 1)
+    V.wait_ge(S.v_me, 1)
+    V.quantize_mx(T.qm[:, 0:128], T.sm[:, 0:128], T.mt[:, 0:512]).then_inc(S.v_qme, 1)
+    V.wait_ge(S.t_oe1, 1)
+    V.tensor_copy(T.ys[:, 256:288], T.px[:, 0:125:4]).then_inc(S.v_y, 1)
+    V.tensor_copy(T.ys[:, 480:512], T.px[:, 1:126:4]).then_inc(S.v_y, 1)
+
+    def mm(o, cols, lq, ls, a, rq, rs, c, start, stop):
+        return P.matmul_mx(o[:, 0:cols], lq[:, a:a + 128], ls[:, a:a + 128], rq[:, c:c + cols], rs[:, c:c + cols], start, stop)
+    P.wait_ge(S.v_qu, 1)
+    P.wait_ge(S.v_qx, 1)
+    for k in range(2):
+        mm(pf[k], 256, T.qu, T.su, 128 * k, T.qx, T.sx, 64, True, True).then_inc(S["t_f%d" % k], 1)
+    P.wait_ge(S.v_qs, 1)
+    mm(T.pl, 128, T.qu, T.su, 256, T.qx, T.sx, 64, True, False)
+    mm(T.pl, 128, T.qu, T.su, 384, T.qx, T.sx, 64 + TC - H, False, True).then_inc(S.t_l, 1)
+    P.wait_ge(S.v_e, 4)
+    for b in range(4):
+        mm(pv[b], 256, T.qi, T.si, 128 * b, T.qx, T.sx, 64, True, True).then_inc(S["t_v%d" % b], 1)
+    P.wait_ge(S.arr, arrivals)
+    P.wait_ge(S.v_d, 4)
+    off = H if first or last else 0
+    for b in range(4):
+        mm(pv[b], 128, T.qi, T.si, 128 * b, T.qx, T.sx, off, True, True).then_inc(S["t_lv%d" % b], 1)
+    P.wait_ge(S.v_qw, 1)
+    P.wait_ge(S.v_qm, 1)
+    for o in range(2):
+        mm(pf[o], 382, T.qw, T.sw, 128 * o, T.qm, T.sm, 128, True, False)
+        mm(pf[o], 382, T.qw, T.sw, 256 + 128 * o, T.qm, T.sm, 130, False, True).then_inc(S["t_oi%d" % o], 1)
+    P.wait_ge(S.v_qme, 1)
+    pe = [T.pl, T.px]
+    for o in range(2):
+        mm(pe[o], 128, T.qw, T.sw, 128 * o, T.qm, T.sm, 0, True, False)
+        mm(pe[o], 128, T.qw, T.sw, 256 + 128 * o, T.qm, T.sm, 2, False, True).then_inc(S["t_oe%d" % o], 1)
+
+    C.wait_ge(S.v_ss, 1)
+    C.wait_ge(S.v_u1, 4)
+    for k in range(2):
+        for h in range(2):
+            C.activation(T.ss[:, h, :, 8 * k + 4 * h:8 * k + 4 * h + 4, :], T.us[:, k, :, 0:4, :], CP).then_inc(S.s_ss, 1)
+    for b in range(4):
+        C.wait_ge(S["t_v%d" % b], 1)
+        C.activation(T.vw[:, b:1024:4], pv[b][:, 0:256], CP).then_inc(S["s_v%d" % b], 1)
+    C.wait_ge(S.v_f, 4)
+    for t in range(4):
+        C.activation(T.fx[:, 512 + t:2048:4], T.fc[:, 128:512], CP).then_inc(S.s_x, 1)
+    for b in range(4):
+        C.wait_ge(S["s_v%d" % b], 1)
+    C.activation(T.vw[:, 1280:1536], T.vw[:, 0:256], CP).then_inc(S.s_vc, 1)
+    C.wait_ge(S.v_fe, 4)
+    for t in range(4):
+        C.activation(T.fx[:, t:512:4], T.fc[:, 0:128], CP).then_inc(S.s_xe, 1)
+    C.wait_ge(S.v_d, 4)
+    C.activation(T.dw[:, 1280:1536], T.dw[:, 0:256], CP).then_inc(S.s_dc, 1)
+    if first or last:
+        C.wait_ge(S.v_hz, 2)
+    for b in range(4):
+        C.wait_ge(S["t_lv%d" % b], 1)
+        if last:
+            C.activation(T.vw[:, 1152 + b:1280:4], pv[b][:, 0:32], CP).then_inc(S["s_lv%d" % b], 1)
+        elif first:
+            C.activation(T.vw[:, 1024 + b:1152:4], pv[b][:, 0:32], CP).then_inc(S["s_lv%d" % b], 1)
+        else:
+            C.activation(T.vw[:, 1024 + b:1280:4], pv[b][:, 0:64], CP).then_inc(S["s_lv%d" % b], 1)
+    for o in range(2):
+        C.wait_ge(S["t_oi%d" % o], 1)
+        C.activation(T.ys[:, 256 * o + 32:256 * o + 128], pf[o][:, 0:382:4], CP).then_inc(S.s_y, 1)
+        C.activation(T.ys[:, 256 * o + 128:256 * o + 224], pf[o][:, 1:382:4], CP).then_inc(S.s_y, 1)
+    C.wait_ge(S.t_oe0, 1)
+    C.activation(T.ys[:, 0:32], T.pl[:, 0:125:4], CP).then_inc(S.s_ye, 1)
+    C.activation(T.ys[:, 224:256], T.pl[:, 1:126:4], CP).then_inc(S.s_ye, 1)
+    C.wait_ge(S.v_y, 2)
+    C.dma_start(T.y[:, 480:512], T.ys[:, 480:512]).then_inc(S.st2, 16)
+    C.wait_ge(S.st2, 16)
+
+    Y.wait_ge(S.s_y, 4)
+    for o in range(2):
+        Y.dma_start(T.y[:, 256 * o + 32:256 * o + 224], T.ys[:, 256 * o + 32:256 * o + 224]).then_inc(S.st1, 16)
+    Y.wait_ge(S.s_ye, 2)
+    Y.dma_start(T.y[:, 0:32], T.ys[:, 0:32]).then_inc(S.st1, 16)
+    Y.wait_ge(S.v_y, 2)
+    Y.dma_start(T.y[:, 224:288], T.ys[:, 224:288]).then_inc(S.st1, 16)
+    Y.wait_ge(S.st1, 64)

@@ -1,72 +1,31 @@
 from concourse.bass import DstId, RemoteDMATransfer
 from concourse.mybir import dt, AluOpType, ActivationFunctionType
 
-H = 32
-TC = 256
-CL = 31
+H, TC, CL, PAD = 32, 256, 31, 8
+OWN, EP = 2 * H, TC
+EC = (16, 0, TC - 16, TC - 32)
+IC = (32, 80, 128, 176)
+DUP = TC + 2 * H
+WN = 2 * (DUP + 2 * H)
 SCRATCH = {
-    "xe": ("sbuf", [128, 512], "bfloat16"),
-    "qe": ("sbuf", [128, 128], "float8_e4m3fn_x4"),
-    "se": ("sbuf", [128, 128], "uint8"),
-    "rq": ("sbuf", [128, H], "float8_e4m3fn_x4"),
-    "rs": ("sbuf", [128, H], "uint8"),
-    "xt": ("sbuf", [128, 1408], "bfloat16"),
-    "qx": ("sbuf", [128, 416], "float8_e4m3fn_x4"),
-    "sx": ("sbuf", [128, 416], "uint8"),
     "ub": ("sbuf", [128, 2, 8, 4], "bfloat16"),
     "us": ("sbuf", [128, 2, 8, 16, 4], "bfloat16"),
-    "ss": ("sbuf", [128, 2, 8, 16, 4], "bfloat16"),
-    "qu": ("sbuf", [128, 512], "float8_e4m3fn_x4"),
-    "su": ("sbuf", [128, 512], "uint8"),
-    "one": ("sbuf", [128, 516], "bfloat16"),
-    "eye": ("sbuf", [128, 516], "bfloat16"),
-    "qi": ("sbuf", [128, 512], "float8_e4m3fn_x4"),
-    "si": ("sbuf", [128, 512], "uint8"),
-    "wb": ("sbuf", [128, 2048], "bfloat16"),
-    "qw": ("sbuf", [128, 512], "float8_e4m3fn_x4"),
-    "sw": ("sbuf", [128, 512], "uint8"),
-    "pi": ("sbuf", [128, 1], "int32"),
-    "ti": ("sbuf", [128, 1], "int32"),
-    "h4": ("sbuf", [128, 1], "int32"),
-    "tq": ("sbuf", [128, 1], "float32"),
-    "te": ("sbuf", [128, 1], "float32"),
-    "tl": ("sbuf", [128, 1], "float32"),
-    "hi": ("sbuf", [128, 1], "float32"),
-    "he": ("sbuf", [128, 1], "float32"),
-    "lim": ("sbuf", [128, 1], "float32"),
-    "ic": ("sbuf", [128, 128], "float32"),
-    "tab": ("sbuf", [128, 128], "float32"),
-    "nl": ("sbuf", [128, 128], "int32"),
-    "wl": ("sbuf", [128, 128], "float32"),
-    "lst": ("sbuf", [128, 128], "uint16"),
-    "fa": ("sbuf", [128, 512], "float32"),
-    "fn": ("sbuf", [128, 512], "int32"),
-    "fc": ("sbuf", [128, 512], "float32"),
-    "fx": ("sbuf", [128, 2048], "float32"),
-    "vw": ("sbuf", [128, 1536], "float32"),
-    "dw": ("sbuf", [128, 1536], "float32"),
-    "pr": ("sbuf", [128, 2048], "float32"),
-    "mt": ("sbuf", [128, 2048], "bfloat16"),
-    "qm": ("sbuf", [128, 512], "float8_e4m3fn_x4"),
-    "sm": ("sbuf", [128, 512], "uint8"),
-    "ys": ("sbuf", [128, 512], "float32"),
-    "pf0": ("psum", [128, 512], "float32"),
-    "pf1": ("psum", [128, 512], "float32"),
-    "pl": ("psum", [128, 512], "float32"),
-    "pv0": ("psum", [128, 512], "float32"),
-    "pv1": ("psum", [128, 512], "float32"),
-    "pv2": ("psum", [128, 512], "float32"),
-    "pv3": ("psum", [128, 512], "float32"),
-    "px": ("psum", [128, 512], "float32"),
+    "zt": ("sbuf", [128, 9, 16, 4], "bfloat16"),
 }
-SEMAPHORES = (["d_xe", "d_u", "d_x", "d_w", "st1", "st2", "ra", "rb", "arr", "loc", "g_p", "g_e", "g_c"]
-              + ["v_ones", "v_xp", "v_ss", "v_hz", "v_c1", "v_c2", "v_c3", "v_tab", "v_e", "v_qe", "v_u1", "v_u2", "v_u3",
-                 "v_qu", "v_qx", "v_qs", "v_a", "v_n", "v_l1", "v_l2", "v_l3", "v_f", "v_fe", "v_d", "v_qw", "v_p", "v_m",
-                 "v_qm", "v_dl", "v_pe", "v_me", "v_qme", "v_y"]
-              + ["s_ss", "s_vc", "s_x", "s_dc", "s_xe", "s_y", "s_ye"]
-              + ["s_v%d" % b for b in range(4)] + ["s_lv%d" % b for b in range(4)]
-              + ["t_f0", "t_f1", "t_l", "t_oi0", "t_oi1", "t_oe0", "t_oe1"]
-              + ["t_v%d" % b for b in range(4)] + ["t_lv%d" % b for b in range(4)])
+for names, width, kind in (("qp", 384, "q"), ("rq", H, "q"), ("qx", 320, "q"), ("qu", 256, "q"), ("qz", 144, "q"), ("qi qw qm", 512, "q"),
+                           ("sp", 384, "s"), ("rs", H, "s"), ("sx", 320, "s"), ("su", 256, "s"), ("sz", 144, "s"), ("si sw sm", 512, "s"),
+                           ("xe", 512, "b"), ("xp xt", 1024, "b"), ("one eye", 516, "b"), ("wb mt", 2048, "b"),
+                           ("pi b0 b1 b3", 1, "i"), ("nl", 64, "i"), ("fn", 512, "i"), ("z0 z1 hj hf hi he lim", 1, "f"), ("ic", 48, "f"),
+                           ("tab dc eq wl we wz", 64, "f"), ("lv ld", 64, "u"), ("zf gi", 2048, "f"), ("v0 v1", WN, "f"),
+                           ("d0 d1", WN + 2 * PAD, "f"), ("pr", 1024, "f"), ("ys", 512, "f"),
+                           ("pf0 pf1 pl px pv0 pv1 pv2 pv3", 512, "p")):
+    for name in names.split():
+        SCRATCH[name] = ("psum" if kind == "p" else "sbuf", [128, width],
+                         {"q": "float8_e4m3fn_x4", "s": "uint8", "b": "bfloat16", "i": "int32", "u": "uint16"}.get(kind, "float32"))
+SEMAPHORES = ("d_xe d_u d_x d_w st1 st2 ra rb arr loc g_p g_e g_c v_ones v_xp v_zt v_hz v_c1 v_c2 v_c3 v_c4 v_tab v_e v_qe v_u1 v_u2 v_u3 "
+              "v_qu v_qp v_qx v_qz v_xi v_n0 v_n1 v_f0 v_f1 v_dc v_eq v_nl v_wl v_we v_wz v_lv v_ld v_qw v_p v_sa v_sb v_ma v_mb v_qa v_qb "
+              "v_pe v_se v_me v_qme v_y s_z s_zt s_xe s_xi s_fi s_fe s_vd s_dd s_va s_vb s_ga s_gb s_vg s_ge s_y s_ye t_f0 t_f1 t_l t_oa0 "
+              "t_oa1 t_ob0 t_ob1 t_oe0 t_oe1").split() + [p + str(b) for p in ("s_v", "s_lv", "v_d", "v_dl", "t_v", "t_lv") for b in range(4)]
 
 
 def mask_of(engines):
@@ -83,10 +42,8 @@ def routes(T, topo, core):
         cand = [c for c in topo.cores_of(core) if c != core and topo.may_write(c, dst)]
         cand.sort(key=lambda c: (topo.die(c) != topo.die(core), c))
         relay = cand[side]
-        near = topo.engines(core, relay)[4 * side:4 * side + 4]
-        far = topo.engines(relay, dst)[::2]
-        land = H if side == 1 or nb == 0 else 0
-        out.append((side, relay, dst, near, far, H * side, land))
+        out.append((side, relay, dst, topo.engines(core, relay)[4 * side:4 * side + 4], topo.engines(relay, dst)[::2], EP + H * side,
+                    H if side == 1 or nb == 0 else 0))
     return out
 
 
@@ -100,8 +57,7 @@ def relay_program(g, core, T, topo):
             rid, pid = topo.addr(dst, core)
             m = mask_of(far)
             g.wait_ge(T.sem.ra, len(near))
-            g.remote_dma(T.qx[:, land:land + H].bitcast(dt.uint8), T.rq[:, 0:H].bitcast(dt.uint8), T.sem.arr, T.sem.loc,
-                         pid, rid, m)
+            g.remote_dma(T.qx[:, land:land + H].bitcast(dt.uint8), T.rq[:, 0:H].bitcast(dt.uint8), T.sem.arr, T.sem.loc, pid, rid, m)
             g.wait_ge(T.sem.rb, len(near))
             g.remote_dma(T.sx[:, land:land + H], T.rs[:, 0:H], T.sem.arr, T.sem.loc, pid, rid, m)
             g.wait_ge(T.sem.loc, 2 * len(far))
@@ -114,223 +70,256 @@ def rank_program(g, core, T, topo):
         return
     n = len(T.cores)
     first, last = rank == 0, rank == n - 1
-    S = T.sem
-    A = AluOpType
-    CP = ActivationFunctionType.Copy
+    end = first or last
+    S, A, CP = T.sem, AluOpType, ActivationFunctionType.Copy
     V, C, P, Y = g.vector, g.scalar, g.tensor, g.sync
     pv = [T["pv%d" % b] for b in range(4)]
-    pf = [T.pf0, T.pf1]
+    pf, vw, dw, TO = [T.pf0, T.pf1], [T.v0, T.v1], [T.d0, T.d1], (1, 3, 0, 2)
     out = routes(T, topo, core)
-    arrivals = 0
-    for nb in (rank - 1, rank + 1):
-        if 0 <= nb < n:
-            arrivals += sum(2 * len(q[4]) for q in routes(T, topo, T.cores[nb]) if q[2] == core)
 
+    def waits(q, *pairs):
+        for name in pairs:
+            a, _, c = name.partition(":")
+            q.wait_ge(S[a], int(c or 1))
+
+    def group(call, to, cols, src, at, *more):
+        return call(T.xp[:, 4 * to:4 * (to + cols)], src[:, 4 * at:4 * (at + cols)], *more)
+    arrivals = sum(2 * len(q[4]) for nb in (rank - 1, rank + 1) if 0 <= nb < n for q in routes(T, topo, T.cores[nb]) if q[2] == core)
     Y.dma_start(T.xe[:, 0:4 * H], T.x[:, 0:4 * H]).then_inc(S.d_xe, 16)
     C.dma_start(T.xe[:, 4 * H:8 * H], T.x[:, 4 * (TC - H):4 * TC]).then_inc(S.d_xe, 16)
     Y.dma_start(T.ub[:], T.u[:, 0:64]).then_inc(S.d_u, 16)
-    C.dma_start(T.xt[:, 0:1024], T.x[:]).then_inc(S.d_x, 16)
-    C.dma_start(T.xt[:, 1024:1408], T.x[:, 512:896]).then_inc(S.d_x, 16)
-    Y.wait_ge(S.d_x, 32)
+    Y.dma_start(T.xt[:], T.x[:]).then_inc(S.d_x, 16)
+    Y.wait_ge(S.d_x, 16)
     Y.dma_start(T.wb[:], T.w[:]).then_inc(S.d_w, 16)
-
     g.iota(T.pi[:], [[0, 1]], 0, 1).then_inc(S.g_p, 1)
     g.wait_ge(S.v_ones, 1)
     g.affine_select(T.eye[:], T.one[:], [[-1, 516]], A.is_equal, 0.0, 4, 4).then_inc(S.g_e, 1)
-    g.iota(T.ic[:], [[1, 128]], 0, 0, allow_small_or_imprecise_dtypes=True).then_inc(S.g_c, 1)
+    g.iota(T.ic[:], [[1, 48]], 0, 0, allow_small_or_imprecise_dtypes=True).then_inc(S.g_c, 1)
     g.wait_ge(S.v_qe, 1)
     codes, planes = [], []
     for side, relay, dst, near, far, col, land in out:
         rid, pid = topo.addr(relay, core)
         to = [DstId(rid=rid, pnc=pid)]
         codes.append(RemoteDMATransfer(dst_ids=to, dma_engine_mask=mask_of(near), remote_sem=S.ra,
-                                       src=T.qe[:, col:col + H].bitcast(dt.uint8), dst=T.rq[:, 0:H].bitcast(dt.uint8)))
+                                       src=T.qp[:, col:col + H].bitcast(dt.uint8), dst=T.rq[:, 0:H].bitcast(dt.uint8)))
         planes.append(RemoteDMATransfer(dst_ids=to, dma_engine_mask=mask_of(near), remote_sem=S.rb,
-                                        src=T.se[:, col:col + H], dst=T.rs[:, 0:H]))
+                                        src=T.sp[:, col:col + H], dst=T.rs[:, 0:H]))
     g.remote_dma_fused(codes, local_sem=S.loc)
     g.remote_dma_fused(planes, local_sem=S.loc)
     g.wait_ge(S.loc, sum(2 * len(q[3]) for q in out))
-
     V.memset(T.one[:], 1.0).then_inc(S.v_ones, 1)
     V.memset(T.xe[:, 8 * H:512], 0.0).then_inc(S.v_xp, 1)
-    V.memset(T.ss[:], 0.0).then_inc(S.v_ss, 1)
-    gap = (4 * (TC + H - 1), 4 * (TC + 2 * H)) if first else (4 * (TC - 1), 4 * (TC + H))
-    if first or last:
-        V.memset(T.vw[:, gap[0] + 4:gap[1]], 0.0).then_inc(S.v_hz, 1)
-        V.memset(T.dw[:, gap[0]:gap[1]], 0.0).then_inc(S.v_hz, 1)
-    V.wait_ge(S.g_p, 1)
-    V.tensor_scalar(T.ti[:], T.pi[:], 3, None, A.bitwise_and).then_inc(S.v_c1, 1)
-    V.tensor_scalar(T.h4[:], T.pi[:], 4, None, A.bitwise_and).then_inc(S.v_c1, 1)
-    V.wait_ge(S.v_c1, 2)
-    V.tensor_scalar(T.tq[:], T.ti[:], 0.25, None, A.mult).then_inc(S.v_c2, 1)
-    V.tensor_scalar(T.te[:], T.ti[:], 0.25, float(TC + 2 * H), A.mult, A.add).then_inc(S.v_c2, 1)
-    if first or last:
-        V.tensor_scalar(T.tl[:], T.ti[:], 1.0, 4.0 * (TC + 2 * H) if first else 4.0 * (TC - 1) + 4000.0, A.mult,
-                        A.add).then_inc(S.v_c2, 1)
-    V.wait_ge(S.v_c2, 3 if first or last else 2)
-    V.tensor_scalar(T.hi[:], T.h4[:], 24.0, T.tq[:], A.mult, A.add).then_inc(S.v_c3, 1)
-    V.tensor_scalar(T.he[:], T.h4[:], -24.0, T.te[:], A.mult, A.add).then_inc(S.v_c3, 1)
-    if first or last:
-        V.tensor_scalar(T.lim[:], T.h4[:], -1.0 * (TC + 2 * H) if first else -1000.0, T.tl[:], A.mult,
-                        A.add).then_inc(S.v_c3, 1)
-    V.wait_ge(S.g_e, 1)
-    for b in range(4):
-        V.quantize_mx(T.qi[:, 128 * b:128 * b + 128], T.si[:, 128 * b:128 * b + 128],
-                      T.eye[:, 4 - b:516 - b]).then_inc(S.v_e, 1)
-    V.wait_ge(S.v_xp, 1)
-    V.wait_ge(S.d_xe, 32)
-    V.quantize_mx(T.qe[:], T.se[:], T.xe[:]).then_inc(S.v_qe, 1)
-    V.wait_ge(S.d_u, 16)
+    V.memset(T.zt[:], 0.0).then_inc(S.v_zt, 1)
+    hz = 6 if end else 2
+    for i in range(2):
+        V.memset(dw[i][:, 0:2 * PAD], 0.0).then_inc(S.v_hz, 1)
+        if end:
+            a, e = (TC + H - 1, DUP) if first else (TC - 1, TC + H)
+            V.memset(vw[i][:, 2 * a + 2:2 * e], 0.0).then_inc(S.v_hz, 1)
+            V.memset(dw[i][:, 2 * (a + PAD):2 * (e + PAD)], 0.0).then_inc(S.v_hz, 1)
+    waits(V, "g_p")
+    for b, bit in ((T.b0, 1), (T.b1, 2), (T.b3, 8)):
+        V.tensor_scalar(b[:], T.pi[:], bit, None, A.bitwise_and).then_inc(S.v_c1, 1)
+    waits(V, "v_c1:3")
+    V.tensor_scalar(T.z0[:], T.b0[:], 0.5, float(PAD), A.mult, A.add).then_inc(S.v_c2, 1)
+    V.tensor_scalar(T.z1[:], T.b0[:], 0.5, float(PAD + TC - 1 + 1000), A.mult, A.add).then_inc(S.v_c2, 1)
+    waits(V, "v_c2:2")
+    V.tensor_scalar(T.hj[:], T.b1[:], 24.0, T.z0[:], A.mult, A.add).then_inc(S.v_c3, 1)
+    V.tensor_scalar(T.hf[:], T.b1[:], -8.0, T.z0[:], A.mult, A.add).then_inc(S.v_c3, 1)
+    V.tensor_scalar(T.lim[:], T.b3[:], -125.0, T.z1[:], A.mult, A.add).then_inc(S.v_c4, 1)
+    waits(V, "v_c3:2")
+    V.tensor_scalar(T.hi[:], T.b3[:], 12.0, T.hj[:], A.mult, A.add).then_inc(S.v_c4, 1)
+    V.tensor_scalar(T.he[:], T.b3[:], 28.0 if first else -12.0, T.hf[:], A.mult, A.add).then_inc(S.v_c4, 1)
+
+    def eyes(bs):
+        for b in bs:
+            V.quantize_mx(T.qi[:, 128 * b:128 * b + 128], T.si[:, 128 * b:128 * b + 128], T.eye[:, 4 - b:516 - b]).then_inc(S.v_e, 1)
+    waits(V, "g_e")
+    eyes((1, 3))
+    waits(V, "v_xp", "d_xe:32")
+    V.quantize_mx(T.qp[:, EP:EP + 128], T.sp[:, EP:EP + 128], T.xe[:]).then_inc(S.v_qe, 1)
+    waits(V, "d_u:16")
     for q in range(4):
         V.tensor_copy(T.us[:, :, :, q, :], T.ub[:]).then_inc(S.v_u1, 1)
-    V.wait_ge(S.v_u1, 4)
+    eyes((0,))
+    waits(V, "v_u1:4")
     V.tensor_copy(T.us[:, :, :, 4:8, :], T.us[:, :, :, 0:4, :]).then_inc(S.v_u2, 1)
-    V.wait_ge(S.v_u2, 1)
+    eyes((2,))
+    waits(V, "v_u2")
     V.tensor_copy(T.us[:, :, :, 8:16, :], T.us[:, :, :, 0:8, :]).then_inc(S.v_u3, 1)
-    V.wait_ge(S.v_c3, 3 if first or last else 2)
-    V.wait_ge(S.g_c, 1)
-    V.tensor_scalar(T.tab[:, 0:32], T.ic[:, 0:32], T.he[:], None, A.add).then_inc(S.v_tab, 1)
-    V.tensor_scalar(T.tab[:, 32:128], T.ic[:, 32:128], T.hi[:], None, A.add).then_inc(S.v_tab, 1)
-    V.wait_ge(S.v_u3, 1)
-    V.quantize_mx(T.qu[:, 0:256], T.su[:, 0:256], T.us[:]).then_inc(S.v_qu, 1)
-    V.wait_ge(S.d_x, 32)
-    V.quantize_mx(T.qx[:, 64:416], T.sx[:, 64:416], T.xt[:]).then_inc(S.v_qx, 1)
-    V.wait_ge(S.s_ss, 4)
-    V.quantize_mx(T.qu[:, 256:512], T.su[:, 256:512], T.ss[:]).then_inc(S.v_qs, 1)
+    waits(V, "d_x:16")
+    V.quantize_mx(T.qx[:, OWN:OWN + TC], T.sx[:, OWN:OWN + TC], T.xt[:]).then_inc(S.v_qx, 1)
+    for h in (2, 3):
+        group(V.tensor_copy, 64 * h + 16, 48, T.xt, IC[h]).then_inc(S.v_xi, 1)
+    waits(V, "v_u3")
+    V.quantize_mx(T.qu[:], T.su[:], T.us[:]).then_inc(S.v_qu, 1)
+    waits(V, "v_xi:2", "s_xe:4", "s_xi:2")
+    V.quantize_mx(T.qp[:, 0:TC], T.sp[:, 0:TC], T.xp[:]).then_inc(S.v_qp, 1)
+    waits(V, "s_zt:4")
+    V.quantize_mx(T.qz[:], T.sz[:], T.zt[:]).then_inc(S.v_qz, 1)
+    waits(V, "v_c4:3", "g_c")
+    V.tensor_scalar(T.tab[:, 0:16], T.ic[:, 0:16], T.he[:], float(EC[0] + (0 if first else DUP)), A.add, A.add).then_inc(S.v_tab, 1)
+    V.tensor_scalar(T.tab[:, 16:64], T.ic[:], T.hi[:], float(IC[0]), A.add, A.add).then_inc(S.v_tab, 1)
+
+    def own_d(t):
+        waits(V, "s_v%d" % t)
+        V.tensor_tensor(dw[t % 2][:, 2 * PAD + t // 2:2 * (PAD + TC - 1):2], pv[t][:, 1:TC],
+                        vw[t % 2][:, t // 2:2 * (TC - 1):2], A.subtract).then_inc(S["v_d%d" % t], 1)
+
+    def fr(k):
+        waits(V, "v_n%d" % k)
+        for h in range(4):
+            q = 4 * k + 2 * (h % 2) + 8 * (h // 2)
+            a = 256 * k + 64 * h
+            V.tensor_tensor(T.zf[:, 2 * q + 1:2048:32], pf[k][:, 64 * h:64 * h + 64], T.fn[:, a:a + 64],
+                            A.subtract).then_inc(S["v_f%d" % k], 1)
+    own_d(1)
+    own_d(3)
     for k in range(2):
-        V.wait_ge(S["t_f%d" % k], 1)
-        V.tensor_scalar(T.fa[:, 256 * k:256 * k + 256], pf[k][:, 0:256], -float(CL), float(CL), A.max,
-                        A.min).then_inc(S.v_a, 1)
-        V.tensor_scalar(T.fn[:, 256 * k:256 * k + 256], pf[k][:, 0:256], -float(CL), float(CL), A.max,
-                        A.min).then_inc(S.v_n, 1)
-    V.wait_ge(S.v_a, 2)
-    V.wait_ge(S.v_n, 2)
-    for sem, c0, c1 in ((S.v_f, 32, 128), (S.v_fe, 0, 32)):
-        for k in range(2):
-            for h in range(2):
-                a = 256 * k + (c0 if h == 0 else (TC - H if c0 == 0 else 128))
-                e = a + c1 - c0
-                V.tensor_tensor(T.fc[:, 4 * c0 + 2 * k + h:4 * c1:4], T.fa[:, a:e], T.fn[:, a:e], A.subtract).then_inc(sem, 1)
-    V.wait_ge(S.t_l, 1)
-    V.tensor_scalar(T.nl[:], T.pl[:, 0:128], -float(CL), float(CL), A.max, A.min).then_inc(S.v_l1, 1)
-    V.wait_ge(S.v_tab, 2)
-    V.wait_ge(S.v_l1, 1)
-    V.tensor_tensor(T.wl[:], T.nl[:], T.tab[:], A.add).then_inc(S.v_l2, 1)
-    for b in range(4):
-        V.wait_ge(S["s_v%d" % b], 1)
-        V.tensor_tensor(T.dw[:, b:1020:4], pv[b][:, 1:256], T.vw[:, b:1020:4], A.subtract).then_inc(S.v_d, 1)
-    V.wait_ge(S.v_l2, 1)
-    if first or last:
-        V.tensor_scalar(T.lst[:, 0:32], T.wl[:, 0:32], 4.0, T.lim[:], A.mult, A.max if first else A.min).then_inc(S.v_l3, 1)
-    else:
-        V.tensor_scalar(T.lst[:, 0:32], T.wl[:, 0:32], 4.0, None, A.mult).then_inc(S.v_l3, 1)
-    V.tensor_scalar(T.lst[:, 32:128], T.wl[:, 32:128], 4.0, None, A.mult).then_inc(S.v_l3, 1)
-    V.wait_ge(S.d_w, 16)
+        waits(V, "t_f%d" % k)
+        V.tensor_scalar(T.fn[:, TC * k:TC * k + TC], pf[k][:, 0:TC], -float(CL), float(CL), A.max, A.min).then_inc(S["v_n%d" % k], 1)
+    fr(0)
+    waits(V, "t_l")
+    V.tensor_scalar(T.dc[:], T.pl[:, 0:64], -float(CL), float(CL), A.max, A.min).then_inc(S.v_dc, 1)
+    fr(1)
+    waits(V, "v_dc")
+    V.tensor_copy(T.nl[:], T.dc[:]).then_inc(S.v_nl, 1)
+    V.tensor_tensor(T.eq[:], T.dc[:], T.pl[:, 0:64], A.is_equal).then_inc(S.v_eq, 1)
+    waits(V, "v_tab:2", "v_nl")
+    V.tensor_tensor(T.wl[:], T.nl[:], T.tab[:], A.add).then_inc(S.v_wl, 1)
+    own_d(0)
+    waits(V, "v_wl", "v_eq")
+    wl = T.wl
+    if end:
+        wl = T.we
+        V.tensor_scalar(T.we[:], T.wl[:], T.z0[:] if first else T.lim[:], None, A.max if first else A.min).then_inc(S.v_we, 1)
+        waits(V, "v_we")
+    V.tensor_tensor(T.wz[:], wl[:], T.eq[:], A.mult).then_inc(S.v_wz, 1)
+    V.tensor_scalar(T.lv[:], wl[:], 2.0, -2.0 * PAD, A.mult, A.add).then_inc(S.v_lv, 1)
+    own_d(2)
+    waits(V, "v_wz")
+    V.tensor_scalar(T.ld[:], T.wz[:], 2.0, None, A.mult).then_inc(S.v_ld, 1)
+    di, vi = 2 * (PAD + TC - 1), 2 * (TC - 1)
+    waits(V, "v_ld", "v_lv", "s_fi", "v_hz:%d" % hz, "v_d0", "v_d2")
+    V.tensor_tensor(T.pr[:, 256:1024], T.d0[:, 0:di].indirect(T.ld[:, 16:64]), T.zf[:, 513:2048:2], A.mult).then_inc(S.v_p, 1)
+    waits(V, "d_w:16")
     V.quantize_mx(T.qw[:], T.sw[:], T.wb[:]).then_inc(S.v_qw, 1)
-    V.wait_ge(S.v_l3, 2)
-    V.wait_ge(S.v_d, 4)
-    V.wait_ge(S.s_x, 4)
-    V.tensor_tensor(T.pr[:, 512:2048], T.dw[:, 0:1020].indirect(T.lst[:, 32:128]), T.fx[:, 512:2048], A.mult).then_inc(S.v_p, 1)
-    V.wait_ge(S.v_p, 1)
-    V.tensor_tensor(T.mt[:, 512:2048], T.vw[:, 0:1020].indirect(T.lst[:, 32:128]), T.pr[:, 512:2048], A.add).then_inc(S.v_m, 1)
-    V.wait_ge(S.v_m, 1)
-    V.quantize_mx(T.qm[:, 128:512], T.sm[:, 128:512], T.mt[:, 512:2048]).then_inc(S.v_qm, 1)
-    if first or last:
-        V.wait_ge(S.v_hz, 2)
-    for b in range(4):
-        V.wait_ge(S["s_lv%d" % b], 1)
-        if last:
-            V.tensor_tensor(T.dw[:, 1152 + b:1280:4], pv[b][:, 1:33], T.vw[:, 1152 + b:1280:4], A.subtract).then_inc(S.v_dl, 1)
-        elif first:
-            V.tensor_tensor(T.dw[:, 1020 + b:1148:4], pv[b][:, 0:32], T.vw[:, 1020 + b:1148:4], A.subtract).then_inc(S.v_dl, 1)
-        else:
-            V.tensor_tensor(T.dw[:, 1020 + b:1280:4], pv[b][:, 0:65], T.vw[:, 1020 + b:1280:4], A.subtract).then_inc(S.v_dl, 1)
-    V.wait_ge(S.s_vc, 1)
-    V.wait_ge(S.s_dc, 1)
-    V.wait_ge(S.s_xe, 4)
-    V.wait_ge(S.v_dl, 4)
-    V.tensor_tensor(T.pr[:, 0:512], T.dw[:].indirect(T.lst[:, 0:32]), T.fx[:, 0:512], A.mult).then_inc(S.v_pe, 1)
-    V.wait_ge(S.v_pe, 1)
-    V.tensor_tensor(T.mt[:, 0:512], T.vw[:].indirect(T.lst[:, 0:32]), T.pr[:, 0:512], A.add).then_inc(S.v_me, 1)
-    V.wait_ge(S.v_me, 1)
+    waits(V, "s_z:2")
+    halves = ((16, 40, "a"), (40, 64, "b"))
+    for m0, m1, c in halves:
+        waits(V, "s_v" + c, "s_g" + c)
+        V.tensor_tensor_scan(T.mt[:, 32 * m0:32 * m1], T.zf[:, 32 * m0:32 * m1], T.gi[:, 32 * m0:32 * m1], 0.0,
+                             A.mult, A.add).then_inc(S["v_s" + c], 1)
+    waits(V, "v_p")
+    for m0, m1, c in halves:
+        waits(V, "v_s" + c)
+        V.tensor_tensor(T.mt[:, 32 * m0:32 * m1:2], T.v0[:, 0:vi].indirect(T.lv[:, m0:m1]), T.pr[:, 16 * m0:16 * m1],
+                        A.add).then_inc(S["v_m" + c], 1)
+    for m0, m1, c in halves:
+        waits(V, "v_m" + c)
+        V.quantize_mx(T.qm[:, 8 * m0:8 * m1], T.sm[:, 8 * m0:8 * m1], T.mt[:, 32 * m0:32 * m1]).then_inc(S["v_q" + c], 1)
+    a, e, b = (TC + H, DUP, 1) if last else (TC - 1, TC + H - 1 if first else DUP, 0)
+    for t in TO:
+        waits(V, "s_lv%d" % t)
+        V.tensor_tensor(dw[t % 2][:, 2 * (PAD + a) + t // 2:2 * (PAD + e):2], pv[t][:, b:b + e - a],
+                        vw[t % 2][:, 2 * a + t // 2:2 * e:2], A.subtract).then_inc(S["v_dl%d" % t], 1)
+    waits(V, "s_dd:2", "s_vd:2", "s_fe", "v_dl0", "v_dl2")
+    V.tensor_tensor(T.pr[:, 0:256], T.d0[:].indirect(T.ld[:, 0:16]), T.zf[:, 1:512:2], A.mult).then_inc(S.v_pe, 1)
+    waits(V, "s_vg", "s_ge")
+    V.tensor_tensor_scan(T.mt[:, 0:512], T.zf[:, 0:512], T.gi[:, 0:512], 0.0, A.mult, A.add).then_inc(S.v_se, 1)
+    waits(V, "v_pe", "v_se")
+    V.tensor_tensor(T.mt[:, 0:512:2], T.v0[:].indirect(T.lv[:, 0:16]), T.pr[:, 0:256], A.add).then_inc(S.v_me, 1)
+    waits(V, "v_me")
     V.quantize_mx(T.qm[:, 0:128], T.sm[:, 0:128], T.mt[:, 0:512]).then_inc(S.v_qme, 1)
-    V.wait_ge(S.t_oe1, 1)
-    V.tensor_copy(T.ys[:, 256:288], T.px[:, 0:125:4]).then_inc(S.v_y, 1)
-    V.tensor_copy(T.ys[:, 480:512], T.px[:, 1:126:4]).then_inc(S.v_y, 1)
+
+    def edge_y(call, o, src, sem):
+        for h in range(4):
+            call(T.ys[:, TC * o + EC[h]:TC * o + EC[h] + 16], src[:, h % 2 + 4 * (h // 2):128:8]).then_inc(sem, 1)
+    waits(V, "t_oe1")
+    edge_y(V.tensor_copy, 1, T.px, S.v_y)
 
     def mm(o, cols, lq, ls, a, rq, rs, c, start, stop):
         return P.matmul_mx(o[:, 0:cols], lq[:, a:a + 128], ls[:, a:a + 128], rq[:, c:c + cols], rs[:, c:c + cols], start, stop)
-    P.wait_ge(S.v_qu, 1)
-    P.wait_ge(S.v_qx, 1)
+    waits(P, "v_e:4", "v_qx")
+    for t in TO:
+        mm(pv[t], TC, T.qi, T.si, 128 * t, T.qx, T.sx, OWN, True, True).then_inc(S["t_v%d" % t], 1)
+    waits(P, "v_qu", "v_qp")
     for k in range(2):
-        mm(pf[k], 256, T.qu, T.su, 128 * k, T.qx, T.sx, 64, True, True).then_inc(S["t_f%d" % k], 1)
-    P.wait_ge(S.v_qs, 1)
-    mm(T.pl, 128, T.qu, T.su, 256, T.qx, T.sx, 64, True, False)
-    mm(T.pl, 128, T.qu, T.su, 384, T.qx, T.sx, 64 + TC - H, False, True).then_inc(S.t_l, 1)
-    P.wait_ge(S.v_e, 4)
-    for b in range(4):
-        mm(pv[b], 256, T.qi, T.si, 128 * b, T.qx, T.sx, 64, True, True).then_inc(S["t_v%d" % b], 1)
+        mm(pf[k], TC, T.qu, T.su, 128 * k, T.qp, T.sp, 0, True, True).then_inc(S["t_f%d" % k], 1)
+    waits(P, "v_qz", "v_qe")
+    for h in range(4):
+        r = mm(T.pl, 128, T.qz, T.sz, 10 - 2 * (h % 2) - 8 * (h // 2), T.qp, T.sp, 64 * h, h == 0, h == 3)
+    r.then_inc(S.t_l, 1)
     P.wait_ge(S.arr, arrivals)
-    P.wait_ge(S.v_d, 4)
-    off = H if first or last else 0
-    for b in range(4):
-        mm(pv[b], 128, T.qi, T.si, 128 * b, T.qx, T.sx, off, True, True).then_inc(S["t_lv%d" % b], 1)
-    P.wait_ge(S.v_qw, 1)
-    P.wait_ge(S.v_qm, 1)
-    for o in range(2):
-        mm(pf[o], 382, T.qw, T.sw, 128 * o, T.qm, T.sm, 128, True, False)
-        mm(pf[o], 382, T.qw, T.sw, 256 + 128 * o, T.qm, T.sm, 130, False, True).then_inc(S["t_oi%d" % o], 1)
-    P.wait_ge(S.v_qme, 1)
-    pe = [T.pl, T.px]
-    for o in range(2):
-        mm(pe[o], 128, T.qw, T.sw, 128 * o, T.qm, T.sm, 0, True, False)
-        mm(pe[o], 128, T.qw, T.sw, 256 + 128 * o, T.qm, T.sm, 2, False, True).then_inc(S["t_oe%d" % o], 1)
+    for t in TO:
+        waits(P, "v_d%d" % t)
+        mm(pv[t], 128, T.qi, T.si, 128 * t, T.qx, T.sx, H if end else 0, True, True).then_inc(S["t_lv%d" % t], 1)
+    waits(P, "v_qw", "v_f0:4", "v_f1:4")
+    inner = (pf, [pv[0], pv[2]])
+    for i, (m0, m1, c) in enumerate(halves):
+        waits(P, "v_q" + c)
+        if i == 1:
+            waits(P, "s_lv0", "v_dl0", "s_lv2", "v_dl2")
+        for o in range(2):
+            mm(inner[i][o], 190, T.qw, T.sw, 128 * o, T.qm, T.sm, 8 * m0, True, False)
+            mm(inner[i][o], 190, T.qw, T.sw, 256 + 128 * o, T.qm, T.sm, 8 * m0 + 2, False, True).then_inc(S["t_o%s%d" % (c, o)], 1)
+    waits(P, "v_dc", "v_eq", "v_qme")
+    for o, pe in enumerate((T.pl, T.px)):
+        mm(pe, 128, T.qw, T.sw, 128 * o, T.qm, T.sm, 0, True, False)
+        mm(pe, 128, T.qw, T.sw, 256 + 128 * o, T.qm, T.sm, 2, False, True).then_inc(S["t_oe%d" % o], 1)
 
-    C.wait_ge(S.v_ss, 1)
-    C.wait_ge(S.v_u1, 4)
+    waits(C, "v_ones")
+    for i in range(2):
+        C.activation(T.zf[:, 1024 * i:1024 * i + 1024:2], T.one[:, 0:512], CP, 0.0, 0.0).then_inc(S.s_z, 1)
+    waits(C, "v_zt", "d_u:16")
     for k in range(2):
-        for h in range(2):
-            C.activation(T.ss[:, h, :, 8 * k + 4 * h:8 * k + 4 * h + 4, :], T.us[:, k, :, 0:4, :], CP).then_inc(S.s_ss, 1)
-    for b in range(4):
-        C.wait_ge(S["t_v%d" % b], 1)
-        C.activation(T.vw[:, b:1024:4], pv[b][:, 0:256], CP).then_inc(S["s_v%d" % b], 1)
-    C.wait_ge(S.v_f, 4)
-    for t in range(4):
-        C.activation(T.fx[:, 512 + t:2048:4], T.fc[:, 128:512], CP).then_inc(S.s_x, 1)
-    for b in range(4):
-        C.wait_ge(S["s_v%d" % b], 1)
-    C.activation(T.vw[:, 1280:1536], T.vw[:, 0:256], CP).then_inc(S.s_vc, 1)
-    C.wait_ge(S.v_fe, 4)
-    for t in range(4):
-        C.activation(T.fx[:, t:512:4], T.fc[:, 0:128], CP).then_inc(S.s_xe, 1)
-    C.wait_ge(S.v_d, 4)
-    C.activation(T.dw[:, 1280:1536], T.dw[:, 0:256], CP).then_inc(S.s_dc, 1)
-    if first or last:
-        C.wait_ge(S.v_hz, 2)
-    for b in range(4):
-        C.wait_ge(S["t_lv%d" % b], 1)
-        if last:
-            C.activation(T.vw[:, 1152 + b:1280:4], pv[b][:, 0:32], CP).then_inc(S["s_lv%d" % b], 1)
-        elif first:
-            C.activation(T.vw[:, 1024 + b:1152:4], pv[b][:, 0:32], CP).then_inc(S["s_lv%d" % b], 1)
-        else:
-            C.activation(T.vw[:, 1024 + b:1280:4], pv[b][:, 0:64], CP).then_inc(S["s_lv%d" % b], 1)
+        for e in range(2):
+            C.activation(T.zt[:, 0:8, 10 + 4 * k + e, :], T.ub[:, k, :, :], CP).then_inc(S.s_zt, 1)
+    waits(C, "d_xe:32")
+    for h in range(4):
+        group(C.activation, 64 * h, 16, T.xe, EC[h] if EC[h] < H else EC[h] - (TC - 2 * H), CP).then_inc(S.s_xe, 1)
+    waits(C, "d_x:16")
+    for h in range(2):
+        group(C.activation, 64 * h + 16, 48, T.xt, IC[h], CP).then_inc(S.s_xi, 1)
+    for t in TO:
+        waits(C, "t_v%d" % t)
+        C.activation(vw[t % 2][:, t // 2:2 * TC:2], pv[t][:, 0:TC], CP).then_inc(S["s_v%d" % t], 1)
+    waits(C, "v_f0:4", "v_f1:4")
+    C.activation(T.zf[:, 515:2048:4], T.zf[:, 513:2048:4], CP).then_inc(S.s_fi, 1)
+    waits(C, "s_v1", "s_v3", "v_lv", "v_hz:%d" % hz, "v_d1", "v_d3")
+    for m0, m1, c in halves:
+        C.activation(T.gi[:, 32 * m0 + 1:32 * m1:2], T.v1[:, 0:vi].indirect(T.lv[:, m0:m1]), CP).then_inc(S["s_v" + c], 1)
+        waits(C, "v_ld")
+        C.activation(T.gi[:, 32 * m0:32 * m1:2], T.d1[:, 0:di].indirect(T.ld[:, m0:m1]), CP).then_inc(S["s_g" + c], 1)
+    C.activation(T.zf[:, 3:512:4], T.zf[:, 1:512:4], CP).then_inc(S.s_fe, 1)
+    waits(C, "s_v0", "s_v2", "v_d0", "v_d2")
+    for i in range(2):
+        C.activation(vw[i][:, 2 * DUP:WN], vw[i][:, 0:4 * H], CP).then_inc(S.s_vd, 1)
+        C.activation(dw[i][:, 2 * (DUP + PAD):WN + 2 * PAD], dw[i][:, 2 * PAD:2 * PAD + 4 * H], CP).then_inc(S.s_dd, 1)
+    ha, he = (TC + H, DUP) if last else (TC, TC + H if first else DUP)
+    for t in TO:
+        waits(C, "t_lv%d" % t)
+        C.activation(vw[t % 2][:, 2 * ha + t // 2:2 * he:2], pv[t][:, 0:he - ha], CP).then_inc(S["s_lv%d" % t], 1)
+    waits(C, "s_vd:2", "s_dd:2", "s_lv1", "s_lv3")
+    C.activation(T.gi[:, 1:512:2], T.v1[:].indirect(T.lv[:, 0:16]), CP).then_inc(S.s_vg, 1)
+    waits(C, "v_dl1", "v_dl3")
+    C.activation(T.gi[:, 0:512:2], T.d1[:].indirect(T.ld[:, 0:16]), CP).then_inc(S.s_ge, 1)
+    for i, (m0, m1, c) in enumerate(halves):
+        for o in range(2):
+            waits(C, "t_o%s%d" % (c, o))
+            for h in range(4):
+                a = TC * o + IC[h] + 24 * i
+                C.activation(T.ys[:, a:a + 24], inner[i][o][:, h % 2 + 4 * (h // 2):190:8], CP).then_inc(S.s_y, 1)
+    waits(C, "t_oe0")
+    edge_y(lambda a, b: C.activation(a, b, CP), 0, T.pl, S.s_ye)
+    waits(C, "v_y:4")
+    C.dma_start(T.y[:, 2 * TC - H:2 * TC], T.ys[:, 2 * TC - H:2 * TC]).then_inc(S.st2, 16)
+    waits(C, "st2:16")
+    waits(Y, "s_y:16")
     for o in range(2):
-        C.wait_ge(S["t_oi%d" % o], 1)
-        C.activation(T.ys[:, 256 * o + 32:256 * o + 128], pf[o][:, 0:382:4], CP).then_inc(S.s_y, 1)
-        C.activation(T.ys[:, 256 * o + 128:256 * o + 224], pf[o][:, 1:382:4], CP).then_inc(S.s_y, 1)
-    C.wait_ge(S.t_oe0, 1)
-    C.activation(T.ys[:, 0:32], T.pl[:, 0:125:4], CP).then_inc(S.s_ye, 1)
-    C.activation(T.ys[:, 224:256], T.pl[:, 1:126:4], CP).then_inc(S.s_ye, 1)
-    C.wait_ge(S.v_y, 2)
-    C.dma_start(T.y[:, 480:512], T.ys[:, 480:512]).then_inc(S.st2, 16)
-    C.wait_ge(S.st2, 16)
-
-    Y.wait_ge(S.s_y, 4)
-    for o in range(2):
-        Y.dma_start(T.y[:, 256 * o + 32:256 * o + 224], T.ys[:, 256 * o + 32:256 * o + 224]).then_inc(S.st1, 16)
-    Y.wait_ge(S.s_ye, 2)
-    Y.dma_start(T.y[:, 0:32], T.ys[:, 0:32]).then_inc(S.st1, 16)
-    Y.wait_ge(S.v_y, 2)
-    Y.dma_start(T.y[:, 224:288], T.ys[:, 224:288]).then_inc(S.st1, 16)
-    Y.wait_ge(S.st1, 64)
+        Y.dma_start(T.y[:, TC * o + H:TC * o + TC - H], T.ys[:, TC * o + H:TC * o + TC - H]).then_inc(S.st1, 16)
+    waits(Y, "s_ye:4")
+    Y.dma_start(T.y[:, 0:H], T.ys[:, 0:H]).then_inc(S.st1, 16)
+    waits(Y, "v_y:4")
+    Y.dma_start(T.y[:, TC - H:TC + H], T.ys[:, TC - H:TC + H]).then_inc(S.st1, 16)
+    waits(Y, "st1:64")

from concourse.bass import DstId, RemoteDMATransfer
from concourse.mybir import dt, AluOpType, ActivationFunctionType

H, TC, CL, PAD = 32, 256, 31, 8
OWN, EP = 2 * H, TC
EC = (16, 0, TC - 16, TC - 32)
IC = (32, 80, 128, 176)
DUP = TC + 2 * H
WN = 2 * (DUP + 2 * H)
SCRATCH = {
    "ub": ("sbuf", [128, 2, 8, 4], "bfloat16"),
    "us": ("sbuf", [128, 2, 8, 16, 4], "bfloat16"),
    "zt": ("sbuf", [128, 9, 16, 4], "bfloat16"),
}
for names, width, kind in (("qp", 384, "q"), ("rq", H, "q"), ("qx", 320, "q"), ("qu", 256, "q"), ("qz", 144, "q"), ("qi qw qm", 512, "q"),
                           ("sp", 384, "s"), ("rs", H, "s"), ("sx", 320, "s"), ("su", 256, "s"), ("sz", 144, "s"), ("si sw sm", 512, "s"),
                           ("xe", 512, "b"), ("xp xt", 1024, "b"), ("one eye", 516, "b"), ("wb mt", 2048, "b"),
                           ("pi b0 b1 b3", 1, "i"), ("nl", 64, "i"), ("fn", 512, "i"), ("z0 z1 hj hf hi he lim", 1, "f"), ("ic", 48, "f"),
                           ("tab dc eq wl we wz", 64, "f"), ("lv ld", 64, "u"), ("zf gi", 2048, "f"), ("v0 v1", WN, "f"),
                           ("d0 d1", WN + 2 * PAD, "f"), ("pr", 1024, "f"), ("ys", 512, "f"),
                           ("pf0 pf1 pl px pv0 pv1 pv2 pv3", 512, "p")):
    for name in names.split():
        SCRATCH[name] = ("psum" if kind == "p" else "sbuf", [128, width],
                         {"q": "float8_e4m3fn_x4", "s": "uint8", "b": "bfloat16", "i": "int32", "u": "uint16"}.get(kind, "float32"))
SEMAPHORES = ("d_xe d_u d_x d_w st1 st2 ra rb arr loc g_p g_e g_c v_ones v_xp v_zt v_hz v_c1 v_c2 v_c3 v_c4 v_tab v_e v_qe v_u1 v_u2 v_u3 "
              "v_qu v_qp v_qx v_qz v_xi v_n0 v_n1 v_f0 v_f1 v_dc v_eq v_nl v_wl v_we v_wz v_lv v_ld v_qw v_p v_sa v_sb v_ma v_mb v_qa v_qb "
              "v_pe v_se v_me v_qme v_y s_z s_zt s_xe s_xi s_fi s_fe s_vd s_dd s_va s_vb s_ga s_gb s_vg s_ge s_y s_ye t_f0 t_f1 t_l t_oa0 "
              "t_oa1 t_ob0 t_ob1 t_oe0 t_oe1").split() + [p + str(b) for p in ("s_v", "s_lv", "v_d", "v_dl", "t_v", "t_lv") for b in range(4)]


def mask_of(engines):
    return sum(1 << e for e in engines)


def routes(T, topo, core):
    r, n = T.rank_of(core), len(T.cores)
    out = []
    for side, nb in ((0, r - 1), (1, r + 1)):
        if not 0 <= nb < n:
            continue
        dst = T.cores[nb]
        cand = [c for c in topo.cores_of(core) if c != core and topo.may_write(c, dst)]
        cand.sort(key=lambda c: (topo.die(c) != topo.die(core), c))
        relay = cand[side]
        out.append((side, relay, dst, topo.engines(core, relay)[4 * side:4 * side + 4], topo.engines(relay, dst)[::2], EP + H * side,
                    H if side == 1 or nb == 0 else 0))
    return out


def relay_program(g, core, T, topo):
    for rc in topo.cores_of(core):
        if T.rank_of(rc) is None:
            continue
        for side, relay, dst, near, far, col, land in routes(T, topo, rc):
            if relay != core:
                continue
            rid, pid = topo.addr(dst, core)
            m = mask_of(far)
            g.wait_ge(T.sem.ra, len(near))
            g.remote_dma(T.qx[:, land:land + H].bitcast(dt.uint8), T.rq[:, 0:H].bitcast(dt.uint8), T.sem.arr, T.sem.loc, pid, rid, m)
            g.wait_ge(T.sem.rb, len(near))
            g.remote_dma(T.sx[:, land:land + H], T.rs[:, 0:H], T.sem.arr, T.sem.loc, pid, rid, m)
            g.wait_ge(T.sem.loc, 2 * len(far))


def rank_program(g, core, T, topo):
    rank = T.rank_of(core)
    if rank is None:
        relay_program(g, core, T, topo)
        return
    n = len(T.cores)
    first, last = rank == 0, rank == n - 1
    end = first or last
    S, A, CP = T.sem, AluOpType, ActivationFunctionType.Copy
    V, C, P, Y = g.vector, g.scalar, g.tensor, g.sync
    pv = [T["pv%d" % b] for b in range(4)]
    pf, vw, dw, TO = [T.pf0, T.pf1], [T.v0, T.v1], [T.d0, T.d1], (1, 3, 0, 2)
    out = routes(T, topo, core)

    def waits(q, *pairs):
        for name in pairs:
            a, _, c = name.partition(":")
            q.wait_ge(S[a], int(c or 1))

    def group(call, to, cols, src, at, *more):
        return call(T.xp[:, 4 * to:4 * (to + cols)], src[:, 4 * at:4 * (at + cols)], *more)
    arrivals = sum(2 * len(q[4]) for nb in (rank - 1, rank + 1) if 0 <= nb < n for q in routes(T, topo, T.cores[nb]) if q[2] == core)
    Y.dma_start(T.xe[:, 0:4 * H], T.x[:, 0:4 * H]).then_inc(S.d_xe, 16)
    C.dma_start(T.xe[:, 4 * H:8 * H], T.x[:, 4 * (TC - H):4 * TC]).then_inc(S.d_xe, 16)
    Y.dma_start(T.ub[:], T.u[:, 0:64]).then_inc(S.d_u, 16)
    Y.dma_start(T.xt[:], T.x[:]).then_inc(S.d_x, 16)
    Y.wait_ge(S.d_x, 16)
    Y.dma_start(T.wb[:], T.w[:]).then_inc(S.d_w, 16)
    g.iota(T.pi[:], [[0, 1]], 0, 1).then_inc(S.g_p, 1)
    g.wait_ge(S.v_ones, 1)
    g.affine_select(T.eye[:], T.one[:], [[-1, 516]], A.is_equal, 0.0, 4, 4).then_inc(S.g_e, 1)
    g.iota(T.ic[:], [[1, 48]], 0, 0, allow_small_or_imprecise_dtypes=True).then_inc(S.g_c, 1)
    g.wait_ge(S.v_qe, 1)
    codes, planes = [], []
    for side, relay, dst, near, far, col, land in out:
        rid, pid = topo.addr(relay, core)
        to = [DstId(rid=rid, pnc=pid)]
        codes.append(RemoteDMATransfer(dst_ids=to, dma_engine_mask=mask_of(near), remote_sem=S.ra,
                                       src=T.qp[:, col:col + H].bitcast(dt.uint8), dst=T.rq[:, 0:H].bitcast(dt.uint8)))
        planes.append(RemoteDMATransfer(dst_ids=to, dma_engine_mask=mask_of(near), remote_sem=S.rb,
                                        src=T.sp[:, col:col + H], dst=T.rs[:, 0:H]))
    g.remote_dma_fused(codes, local_sem=S.loc)
    g.remote_dma_fused(planes, local_sem=S.loc)
    g.wait_ge(S.loc, sum(2 * len(q[3]) for q in out))
    V.memset(T.one[:], 1.0).then_inc(S.v_ones, 1)
    V.memset(T.xe[:, 8 * H:512], 0.0).then_inc(S.v_xp, 1)
    V.memset(T.zt[:], 0.0).then_inc(S.v_zt, 1)
    hz = 6 if end else 2
    for i in range(2):
        V.memset(dw[i][:, 0:2 * PAD], 0.0).then_inc(S.v_hz, 1)
        if end:
            a, e = (TC + H - 1, DUP) if first else (TC - 1, TC + H)
            V.memset(vw[i][:, 2 * a + 2:2 * e], 0.0).then_inc(S.v_hz, 1)
            V.memset(dw[i][:, 2 * (a + PAD):2 * (e + PAD)], 0.0).then_inc(S.v_hz, 1)
    waits(V, "g_p")
    for b, bit in ((T.b0, 1), (T.b1, 2), (T.b3, 8)):
        V.tensor_scalar(b[:], T.pi[:], bit, None, A.bitwise_and).then_inc(S.v_c1, 1)
    waits(V, "v_c1:3")
    V.tensor_scalar(T.z0[:], T.b0[:], 0.5, float(PAD), A.mult, A.add).then_inc(S.v_c2, 1)
    V.tensor_scalar(T.z1[:], T.b0[:], 0.5, float(PAD + TC - 1 + 1000), A.mult, A.add).then_inc(S.v_c2, 1)
    waits(V, "v_c2:2")
    V.tensor_scalar(T.hj[:], T.b1[:], 24.0, T.z0[:], A.mult, A.add).then_inc(S.v_c3, 1)
    V.tensor_scalar(T.hf[:], T.b1[:], -8.0, T.z0[:], A.mult, A.add).then_inc(S.v_c3, 1)
    V.tensor_scalar(T.lim[:], T.b3[:], -125.0, T.z1[:], A.mult, A.add).then_inc(S.v_c4, 1)
    waits(V, "v_c3:2")
    V.tensor_scalar(T.hi[:], T.b3[:], 12.0, T.hj[:], A.mult, A.add).then_inc(S.v_c4, 1)
    V.tensor_scalar(T.he[:], T.b3[:], 28.0 if first else -12.0, T.hf[:], A.mult, A.add).then_inc(S.v_c4, 1)

    def eyes(bs):
        for b in bs:
            V.quantize_mx(T.qi[:, 128 * b:128 * b + 128], T.si[:, 128 * b:128 * b + 128], T.eye[:, 4 - b:516 - b]).then_inc(S.v_e, 1)
    waits(V, "g_e")
    eyes((1, 3))
    waits(V, "v_xp", "d_xe:32")
    V.quantize_mx(T.qp[:, EP:EP + 128], T.sp[:, EP:EP + 128], T.xe[:]).then_inc(S.v_qe, 1)
    waits(V, "d_u:16")
    for q in range(4):
        V.tensor_copy(T.us[:, :, :, q, :], T.ub[:]).then_inc(S.v_u1, 1)
    eyes((0,))
    waits(V, "v_u1:4")
    V.tensor_copy(T.us[:, :, :, 4:8, :], T.us[:, :, :, 0:4, :]).then_inc(S.v_u2, 1)
    eyes((2,))
    waits(V, "v_u2")
    V.tensor_copy(T.us[:, :, :, 8:16, :], T.us[:, :, :, 0:8, :]).then_inc(S.v_u3, 1)
    waits(V, "d_x:16")
    V.quantize_mx(T.qx[:, OWN:OWN + TC], T.sx[:, OWN:OWN + TC], T.xt[:]).then_inc(S.v_qx, 1)
    for h in (2, 3):
        group(V.tensor_copy, 64 * h + 16, 48, T.xt, IC[h]).then_inc(S.v_xi, 1)
    waits(V, "v_u3")
    V.quantize_mx(T.qu[:], T.su[:], T.us[:]).then_inc(S.v_qu, 1)
    waits(V, "v_xi:2", "s_xe:4", "s_xi:2")
    V.quantize_mx(T.qp[:, 0:TC], T.sp[:, 0:TC], T.xp[:]).then_inc(S.v_qp, 1)
    waits(V, "s_zt:4")
    V.quantize_mx(T.qz[:], T.sz[:], T.zt[:]).then_inc(S.v_qz, 1)
    waits(V, "v_c4:3", "g_c")
    V.tensor_scalar(T.tab[:, 0:16], T.ic[:, 0:16], T.he[:], float(EC[0] + (0 if first else DUP)), A.add, A.add).then_inc(S.v_tab, 1)
    V.tensor_scalar(T.tab[:, 16:64], T.ic[:], T.hi[:], float(IC[0]), A.add, A.add).then_inc(S.v_tab, 1)

    def own_d(t):
        waits(V, "s_v%d" % t)
        V.tensor_tensor(dw[t % 2][:, 2 * PAD + t // 2:2 * (PAD + TC - 1):2], pv[t][:, 1:TC],
                        vw[t % 2][:, t // 2:2 * (TC - 1):2], A.subtract).then_inc(S["v_d%d" % t], 1)

    def fr(k):
        waits(V, "v_n%d" % k)
        for h in range(4):
            q = 4 * k + 2 * (h % 2) + 8 * (h // 2)
            a = 256 * k + 64 * h
            V.tensor_tensor(T.zf[:, 2 * q + 1:2048:32], pf[k][:, 64 * h:64 * h + 64], T.fn[:, a:a + 64],
                            A.subtract).then_inc(S["v_f%d" % k], 1)
    own_d(1)
    own_d(3)
    for k in range(2):
        waits(V, "t_f%d" % k)
        V.tensor_scalar(T.fn[:, TC * k:TC * k + TC], pf[k][:, 0:TC], -float(CL), float(CL), A.max, A.min).then_inc(S["v_n%d" % k], 1)
    fr(0)
    waits(V, "t_l")
    V.tensor_scalar(T.dc[:], T.pl[:, 0:64], -float(CL), float(CL), A.max, A.min).then_inc(S.v_dc, 1)
    fr(1)
    waits(V, "v_dc")
    V.tensor_copy(T.nl[:], T.dc[:]).then_inc(S.v_nl, 1)
    V.tensor_tensor(T.eq[:], T.dc[:], T.pl[:, 0:64], A.is_equal).then_inc(S.v_eq, 1)
    waits(V, "v_tab:2", "v_nl")
    V.tensor_tensor(T.wl[:], T.nl[:], T.tab[:], A.add).then_inc(S.v_wl, 1)
    own_d(0)
    waits(V, "v_wl", "v_eq")
    wl = T.wl
    if end:
        wl = T.we
        V.tensor_scalar(T.we[:], T.wl[:], T.z0[:] if first else T.lim[:], None, A.max if first else A.min).then_inc(S.v_we, 1)
        waits(V, "v_we")
    V.tensor_tensor(T.wz[:], wl[:], T.eq[:], A.mult).then_inc(S.v_wz, 1)
    V.tensor_scalar(T.lv[:], wl[:], 2.0, -2.0 * PAD, A.mult, A.add).then_inc(S.v_lv, 1)
    own_d(2)
    waits(V, "v_wz")
    V.tensor_scalar(T.ld[:], T.wz[:], 2.0, None, A.mult).then_inc(S.v_ld, 1)
    di, vi = 2 * (PAD + TC - 1), 2 * (TC - 1)
    waits(V, "v_ld", "v_lv", "s_fi", "v_hz:%d" % hz, "v_d0", "v_d2")
    V.tensor_tensor(T.pr[:, 256:1024], T.d0[:, 0:di].indirect(T.ld[:, 16:64]), T.zf[:, 513:2048:2], A.mult).then_inc(S.v_p, 1)
    waits(V, "d_w:16")
    V.quantize_mx(T.qw[:], T.sw[:], T.wb[:]).then_inc(S.v_qw, 1)
    waits(V, "s_z:2")
    halves = ((16, 40, "a"), (40, 64, "b"))
    for m0, m1, c in halves:
        waits(V, "s_v" + c, "s_g" + c)
        V.tensor_tensor_scan(T.mt[:, 32 * m0:32 * m1], T.zf[:, 32 * m0:32 * m1], T.gi[:, 32 * m0:32 * m1], 0.0,
                             A.mult, A.add).then_inc(S["v_s" + c], 1)
    waits(V, "v_p")
    for m0, m1, c in halves:
        waits(V, "v_s" + c)
        V.tensor_tensor(T.mt[:, 32 * m0:32 * m1:2], T.v0[:, 0:vi].indirect(T.lv[:, m0:m1]), T.pr[:, 16 * m0:16 * m1],
                        A.add).then_inc(S["v_m" + c], 1)
    for m0, m1, c in halves:
        waits(V, "v_m" + c)
        V.quantize_mx(T.qm[:, 8 * m0:8 * m1], T.sm[:, 8 * m0:8 * m1], T.mt[:, 32 * m0:32 * m1]).then_inc(S["v_q" + c], 1)
    a, e, b = (TC + H, DUP, 1) if last else (TC - 1, TC + H - 1 if first else DUP, 0)
    for t in TO:
        waits(V, "s_lv%d" % t)
        V.tensor_tensor(dw[t % 2][:, 2 * (PAD + a) + t // 2:2 * (PAD + e):2], pv[t][:, b:b + e - a],
                        vw[t % 2][:, 2 * a + t // 2:2 * e:2], A.subtract).then_inc(S["v_dl%d" % t], 1)
    waits(V, "s_dd:2", "s_vd:2", "s_fe", "v_dl0", "v_dl2")
    V.tensor_tensor(T.pr[:, 0:256], T.d0[:].indirect(T.ld[:, 0:16]), T.zf[:, 1:512:2], A.mult).then_inc(S.v_pe, 1)
    waits(V, "s_vg", "s_ge")
    V.tensor_tensor_scan(T.mt[:, 0:512], T.zf[:, 0:512], T.gi[:, 0:512], 0.0, A.mult, A.add).then_inc(S.v_se, 1)
    waits(V, "v_pe", "v_se")
    V.tensor_tensor(T.mt[:, 0:512:2], T.v0[:].indirect(T.lv[:, 0:16]), T.pr[:, 0:256], A.add).then_inc(S.v_me, 1)
    waits(V, "v_me")
    V.quantize_mx(T.qm[:, 0:128], T.sm[:, 0:128], T.mt[:, 0:512]).then_inc(S.v_qme, 1)

    def edge_y(call, o, src, sem):
        for h in range(4):
            call(T.ys[:, TC * o + EC[h]:TC * o + EC[h] + 16], src[:, h % 2 + 4 * (h // 2):128:8]).then_inc(sem, 1)
    waits(V, "t_oe1")
    edge_y(V.tensor_copy, 1, T.px, S.v_y)

    def mm(o, cols, lq, ls, a, rq, rs, c, start, stop):
        return P.matmul_mx(o[:, 0:cols], lq[:, a:a + 128], ls[:, a:a + 128], rq[:, c:c + cols], rs[:, c:c + cols], start, stop)
    waits(P, "v_e:4", "v_qx")
    for t in TO:
        mm(pv[t], TC, T.qi, T.si, 128 * t, T.qx, T.sx, OWN, True, True).then_inc(S["t_v%d" % t], 1)
    waits(P, "v_qu", "v_qp")
    for k in range(2):
        mm(pf[k], TC, T.qu, T.su, 128 * k, T.qp, T.sp, 0, True, True).then_inc(S["t_f%d" % k], 1)
    waits(P, "v_qz", "v_qe")
    for h in range(4):
        r = mm(T.pl, 128, T.qz, T.sz, 10 - 2 * (h % 2) - 8 * (h // 2), T.qp, T.sp, 64 * h, h == 0, h == 3)
    r.then_inc(S.t_l, 1)
    P.wait_ge(S.arr, arrivals)
    for t in TO:
        waits(P, "v_d%d" % t)
        mm(pv[t], 128, T.qi, T.si, 128 * t, T.qx, T.sx, H if end else 0, True, True).then_inc(S["t_lv%d" % t], 1)
    waits(P, "v_qw", "v_f0:4", "v_f1:4")
    inner = (pf, [pv[0], pv[2]])
    for i, (m0, m1, c) in enumerate(halves):
        waits(P, "v_q" + c)
        if i == 1:
            waits(P, "s_lv0", "v_dl0", "s_lv2", "v_dl2")
        for o in range(2):
            mm(inner[i][o], 190, T.qw, T.sw, 128 * o, T.qm, T.sm, 8 * m0, True, False)
            mm(inner[i][o], 190, T.qw, T.sw, 256 + 128 * o, T.qm, T.sm, 8 * m0 + 2, False, True).then_inc(S["t_o%s%d" % (c, o)], 1)
    waits(P, "v_dc", "v_eq", "v_qme")
    for o, pe in enumerate((T.pl, T.px)):
        mm(pe, 128, T.qw, T.sw, 128 * o, T.qm, T.sm, 0, True, False)
        mm(pe, 128, T.qw, T.sw, 256 + 128 * o, T.qm, T.sm, 2, False, True).then_inc(S["t_oe%d" % o], 1)

    waits(C, "v_ones")
    for i in range(2):
        C.activation(T.zf[:, 1024 * i:1024 * i + 1024:2], T.one[:, 0:512], CP, 0.0, 0.0).then_inc(S.s_z, 1)
    waits(C, "v_zt", "d_u:16")
    for k in range(2):
        for e in range(2):
            C.activation(T.zt[:, 0:8, 10 + 4 * k + e, :], T.ub[:, k, :, :], CP).then_inc(S.s_zt, 1)
    waits(C, "d_xe:32")
    for h in range(4):
        group(C.activation, 64 * h, 16, T.xe, EC[h] if EC[h] < H else EC[h] - (TC - 2 * H), CP).then_inc(S.s_xe, 1)
    waits(C, "d_x:16")
    for h in range(2):
        group(C.activation, 64 * h + 16, 48, T.xt, IC[h], CP).then_inc(S.s_xi, 1)
    for t in TO:
        waits(C, "t_v%d" % t)
        C.activation(vw[t % 2][:, t // 2:2 * TC:2], pv[t][:, 0:TC], CP).then_inc(S["s_v%d" % t], 1)
    waits(C, "v_f0:4", "v_f1:4")
    C.activation(T.zf[:, 515:2048:4], T.zf[:, 513:2048:4], CP).then_inc(S.s_fi, 1)
    waits(C, "s_v1", "s_v3", "v_lv", "v_hz:%d" % hz, "v_d1", "v_d3")
    for m0, m1, c in halves:
        C.activation(T.gi[:, 32 * m0 + 1:32 * m1:2], T.v1[:, 0:vi].indirect(T.lv[:, m0:m1]), CP).then_inc(S["s_v" + c], 1)
        waits(C, "v_ld")
        C.activation(T.gi[:, 32 * m0:32 * m1:2], T.d1[:, 0:di].indirect(T.ld[:, m0:m1]), CP).then_inc(S["s_g" + c], 1)
    C.activation(T.zf[:, 3:512:4], T.zf[:, 1:512:4], CP).then_inc(S.s_fe, 1)
    waits(C, "s_v0", "s_v2", "v_d0", "v_d2")
    for i in range(2):
        C.activation(vw[i][:, 2 * DUP:WN], vw[i][:, 0:4 * H], CP).then_inc(S.s_vd, 1)
        C.activation(dw[i][:, 2 * (DUP + PAD):WN + 2 * PAD], dw[i][:, 2 * PAD:2 * PAD + 4 * H], CP).then_inc(S.s_dd, 1)
    ha, he = (TC + H, DUP) if last else (TC, TC + H if first else DUP)
    for t in TO:
        waits(C, "t_lv%d" % t)
        C.activation(vw[t % 2][:, 2 * ha + t // 2:2 * he:2], pv[t][:, 0:he - ha], CP).then_inc(S["s_lv%d" % t], 1)
    waits(C, "s_vd:2", "s_dd:2", "s_lv1", "s_lv3")
    C.activation(T.gi[:, 1:512:2], T.v1[:].indirect(T.lv[:, 0:16]), CP).then_inc(S.s_vg, 1)
    waits(C, "v_dl1", "v_dl3")
    C.activation(T.gi[:, 0:512:2], T.d1[:].indirect(T.ld[:, 0:16]), CP).then_inc(S.s_ge, 1)
    for i, (m0, m1, c) in enumerate(halves):
        for o in range(2):
            waits(C, "t_o%s%d" % (c, o))
            for h in range(4):
                a = TC * o + IC[h] + 24 * i
                C.activation(T.ys[:, a:a + 24], inner[i][o][:, h % 2 + 4 * (h // 2):190:8], CP).then_inc(S.s_y, 1)
    waits(C, "t_oe0")
    edge_y(lambda a, b: C.activation(a, b, CP), 0, T.pl, S.s_ye)
    waits(C, "v_y:4")
    C.dma_start(T.y[:, 2 * TC - H:2 * TC], T.ys[:, 2 * TC - H:2 * TC]).then_inc(S.st2, 16)
    waits(C, "st2:16")
    waits(Y, "s_y:16")
    for o in range(2):
        Y.dma_start(T.y[:, TC * o + H:TC * o + TC - H], T.ys[:, TC * o + H:TC * o + TC - H]).then_inc(S.st1, 16)
    waits(Y, "s_ye:4")
    Y.dma_start(T.y[:, 0:H], T.ys[:, 0:H]).then_inc(S.st1, 16)
    waits(Y, "v_y:4")
    Y.dma_start(T.y[:, TC - H:TC + H], T.ys[:, TC - H:TC + H]).then_inc(S.st1, 16)
    waits(Y, "st1:64")
